import numpy as np
import ml_dtypes


def mxq(x, axis, fmt="e4m3"):
    dtype, down = {"e4m3": (ml_dtypes.float8_e4m3fn, 7), "e5m2": (ml_dtypes.float8_e5m2, 14)}[fmt]
    v = np.moveaxis(np.asarray(x, np.float32).astype(ml_dtypes.bfloat16).astype(np.float64), axis, -1)
    blocks = v.reshape(v.shape[:-1] + (-1, 32))
    amax = np.abs(blocks).max(-1, keepdims=True)
    byte = np.maximum(np.where(amax > 0, np.frexp(amax)[1] - 1 + 127, 0) - down, 1)
    scale = np.exp2(byte - 127.0)
    codes = (blocks / scale).astype(np.float32).astype(dtype).astype(np.float64)
    return np.moveaxis((codes * scale).reshape(v.shape), -1, axis)


WIDE = False


def mx_kscale(k):
    if not WIDE:
        return np.ones(k)
    levels = np.array([30, -30])
    if k % 512:
        return np.exp2(np.random.permutation(np.resize(levels, k // 32))).repeat(32)
    a = np.empty((k // 512, 16))
    for p in range(k // 512):
        a[p, :8] = np.random.permutation(np.resize(levels, 8))
        for g in range(8):
            far = levels[np.abs(levels - a[p, g]) >= 10]
            a[p, g + 8] = far[np.random.randint(len(far))]
    return np.exp2(a.ravel()).repeat(32)


def f64(x):
    return np.asarray(x).astype(np.float64)


def striped(idx):
    return np.tile(np.asarray(idx).reshape(-1, 16).T, (8, 1)).astype(np.uint16)


def unstriped(offs):
    return offs[:16].T.reshape(-1).astype(np.int64)


E2M1 = np.array([0.0, 0.5, 1.0, 1.5, 2.0, 3.0, 4.0, 6.0, -0.0, -0.5, -1.0, -1.5, -2.0, -3.0, -4.0, -6.0])


def pack_weight(w, fmt):
    k, n = w.shape
    w = f64(np.asarray(w, np.float32).astype(ml_dtypes.bfloat16)).reshape(k // 32, 32, n)
    amax = np.abs(w).max(1)
    if fmt in ("e4m3", "e5m2"):
        byte = np.frexp(amax)[1] - 1 + 127 - (7 if fmt == "e4m3" else 14)
    else:
        mant, ex = np.frexp(amax / 6.0)
        byte = np.where(mant > 0.5, ex, ex - 1) + 127
    byte = np.clip(np.where(amax > 0, byte, 1), 1, 254)
    scaled = (w * np.exp2(127.0 - byte)[:, None, :]).reshape(k, n).astype(np.float32)
    by_word = np.ascontiguousarray(scaled.reshape(k // 512, 128, 4, n).transpose(0, 1, 3, 2))
    if fmt in ("e4m3", "e5m2"):
        words = by_word.astype(ml_dtypes.float8_e4m3fn if fmt == "e4m3" else ml_dtypes.float8_e5m2).view(np.uint8)
    else:
        c = by_word.astype(ml_dtypes.float4_e2m1fn).view(np.uint8) & 0xF
        words = (c[..., 0::2] | (c[..., 1::2] << 4)).reshape(k // 512, 128, 2 * n)
    return np.ascontiguousarray(words), np.ascontiguousarray(byte.astype(np.uint8).reshape(k // 512, 16, n))


def unpack_weight(words, scales, fmt):
    g, _, n = scales.shape
    words = np.ascontiguousarray(words).reshape(g, 128, n, -1)
    if fmt in ("e4m3", "e5m2"):
        vals = words.view(ml_dtypes.float8_e4m3fn if fmt == "e4m3" else ml_dtypes.float8_e5m2).astype(np.float64)
    else:
        nib = np.empty((g, 128, n, 4), np.uint8)
        nib[..., 0::2] = words & 0xF
        nib[..., 1::2] = words >> 4
        vals = E2M1[nib]
    vals = vals * np.repeat(np.exp2(scales.astype(np.float64) - 127.0), 8, axis=1)[..., None]
    return vals.transpose(0, 1, 3, 2).reshape(g * 512, n)


K, T, Z, J, R, C, O, N, E = 512, 1024, 1024, 256, 512, 512, 256, 256, 1024


def setup_inputs():
    n = np.random.standard_normal
    idx = np.random.permutation(T)[:J]
    idx2 = np.random.permutation(Z)[:J]
    idx3 = np.random.permutation(C)[:J]
    idx4 = np.random.permutation(C)[:J]
    idx5 = np.random.permutation(C)[:O]
    idx6 = np.random.permutation(E)[:O]
    fk = mx_kscale(K)
    fr = mx_kscale(R)
    xtp = pack_weight(n((K, T)) / fk[:, None], "e5m2")
    xop = pack_weight(n((K, Z)) / fk[:, None], "e4m3")
    wp = pack_weight(n((K, R)) * 1 / np.sqrt(K) * fk[:, None] * fr, "e2m1")
    wbp = pack_weight(n((R, N)) * 1 / np.sqrt(R) / fr[:, None], "e2m1")
    return {
        "xt_words": xtp[0],
        "xt_scales": xtp[1],
        "xo_words": xop[0],
        "xo_scales": xop[1],
        "w_words": wp[0],
        "w_scales": wp[1],
        "wb_words": wbp[0],
        "wb_scales": wbp[1],
        "tz": (n((N, E))).astype(np.float32),
        "offs": striped(idx),
        "offs2": striped(idx2),
        "offs3": striped(idx3),
        "offs4": striped(idx4),
        "offs5": striped(idx5),
        "offs6": striped(idx6),
    }


def reference(xt_words, xt_scales, xo_words, xo_scales, w_words, w_scales, wb_words, wb_scales, tz, offs, offs2, offs3, offs4, offs5, offs6):
    idx = unstriped(offs)
    idx2 = unstriped(offs2)
    idx3 = unstriped(offs3)
    idx4 = unstriped(offs4)
    idx5 = unstriped(offs5)
    idx6 = unstriped(offs6)
    xtu = unpack_weight(xt_words, xt_scales, "e5m2")
    xou = unpack_weight(xo_words, xo_scales, "e4m3")
    wu = unpack_weight(w_words, w_scales, "e2m1")
    wbu = unpack_weight(wb_words, wb_scales, "e2m1")
    xtidxg = xtu[:, idx]
    a = wu.T @ xtidxg
    xoidx2g = xou[:, idx2]
    b = wu.T @ xoidx2g
    pw = np.zeros((R, C))
    pw[:, idx3] = a
    pv = np.zeros((R, C))
    pv[:, idx4] = b
    pg = pw + pv
    hid = pg[:, idx5]
    hidq = mxq(hid, 0, "e4m3")
    p = wbu.T @ hidq
    y = p + f64(tz)[:, idx6]
    return y

@@ -1,0 +1,192 @@
+from contextlib import ExitStack
+
+import concourse.mybir as mybir
+
+F32 = mybir.dt.float32
+BF16 = mybir.dt.bfloat16
+I32 = mybir.dt.int32
+U32 = mybir.dt.uint32
+U16 = mybir.dt.uint16
+U8 = mybir.dt.uint8
+E4M3 = mybir.dt.float8_e4m3fn_x4
+E5M2 = mybir.dt.float8_e5m2_x4
+E2M1 = mybir.dt.float4_e2m1fn_x4
+COPY = mybir.ActivationFunctionType.Copy
+ADD = mybir.AluOpType.add
+
+P = 128
+K, T, Z, J, R, C, O, N, E = 512, 1024, 1024, 256, 512, 512, 256, 256, 1024
+PACK = 4
+FLOPS = 2 * K * R * J * 2 + 2 * R * N * O
+
+
+def tile_list_oneforboth_shared_one_tabled_kernel(
+    tc, xt_words, xt_scales, xo_words, xo_scales, w_words, w_scales, wb_words, wb_scales, tz,
+    offs, offs2, offs3, offs4, offs5, offs6, out,
+):
+    nc = tc.nc
+    with ExitStack() as ctx:
+        sb = ctx.enter_context(tc.tile_pool(name="sb", bufs=1))
+        ps = ctx.enter_context(tc.psum_pool(name="ps", bufs=1))
+
+        def tile(name, cols, dtype, tag=None):
+            return sb.tile([P, cols], dtype, name=name, tag=tag or name, align_bytes=64)
+
+        def load_list(name, src):
+            lst = sb.tile([P, J // 16], U16, name=name)
+            nc.sync.dma_start(lst[:], src)
+            return lst
+
+        def load_scales_direct(plane, src):
+            rows = src[0].bitcast(I32)
+            for q in range(4):
+                nc.sync.dma_start(plane[32 * q : 32 * q + 4, :].bitcast(I32), rows[4 * q : 4 * q + 4, :])
+
+        def load_scales_staged(stage, src):
+            rows = src[0].bitcast(I32).rearrange("(q r) c -> r q c", r=4)
+            nc.sync.dma_start(stage[:].rearrange("r (q c) -> r q c", q=4), rows)
+
+        def deal_scales(plane, stage):
+            words = plane[:].bitcast(I32)
+            width = words.shape[1]
+            for q in range(4):
+                nc.vector.tensor_copy(words[32 * q : 32 * q + 4, :], stage[:, q * width : (q + 1) * width])
+
+        xt_stage = sb.tile([4, T], I32, name="xt_stage")
+        xo_stage = sb.tile([4, Z], I32, name="xo_stage")
+        w_stage = sb.tile([4, R], I32, name="w_stage")
+        xt_plane = tile("xt_plane", T, U8)
+        w_plane = tile("w_plane", R, U8)
+        xo_plane = tile("xo_plane", Z, U8)
+        wb_plane = tile("wb_plane", N, U8)
+        nc.gpsimd.memset(wb_plane[:].bitcast(I32), 0)
+        for plane in (w_plane, xt_plane, xo_plane):
+            nc.vector.memset(plane[:].bitcast(I32), 0)
+
+        xt_tab = tile("xt_tab", T, I32)
+        xo_tab = tile("xo_tab", Z, I32)
+        w_raw = tile("w_raw", 2 * R, U8)
+        wb_codes = tile("wb_codes", 2 * N, U8)
+        nc.scalar.dma_start(xt_tab[:], xt_words[0].rearrange("p c r -> p (c r)").bitcast(I32))
+        nc.scalar.dma_start(xo_tab[:], xo_words[0].rearrange("p c r -> p (c r)").bitcast(I32))
+        load_scales_staged(w_stage, w_scales)
+        load_scales_staged(xt_stage, xt_scales)
+        l1 = load_list("l1", offs)
+        nc.sync.dma_start(w_raw[:].bitcast(I32), w_words[0].bitcast(I32))
+        load_scales_staged(xo_stage, xo_scales)
+        l2 = load_list("l2", offs2)
+        l3 = load_list("l3", offs3)
+        l4 = load_list("l4", offs4)
+        l5 = load_list("l5", offs5)
+        l6 = load_list("l6", offs6)
+        nc.sync.dma_start(wb_codes[:].bitcast(I32), wb_words[0].bitcast(I32))
+        load_scales_direct(wb_plane, wb_scales)
+
+        pw = [tile("pw%d" % t, C, F32) for t in range(PACK)]
+        pv = [tile("pv%d" % t, C, F32) for t in range(PACK)]
+        for t in range(PACK):
+            nc.vector.memset(pw[t][:], 0.0)
+        for t in range(PACK):
+            nc.gpsimd.memset(pv[t][:], 0.0)
+
+        w_codes = tile("w_codes", 2 * R, U8)
+        w_scale = tile("w_scale", R, U8)
+        nc.scalar.copy(
+            w_codes[:].bitcast(U16).rearrange("p (t m) -> p t m", t=PACK),
+            w_raw[:].bitcast(U16).rearrange("p (m t) -> p t m", t=PACK),
+        )
+        deal_scales(w_plane, w_stage)
+        deal_scales(xt_plane, xt_stage)
+        nc.vector.tensor_copy(
+            w_scale[:].rearrange("p (t m) -> p t m", t=PACK),
+            w_plane[:].rearrange("p (m t) -> p t m", t=PACK),
+        )
+
+        def gather_packed(name, tab, plane, lst):
+            codes = tile(name + "_codes", J, U32)
+            scale = tile(name + "_scale", J, U8)
+            nc.vector.tensor_copy(scale[:], plane.indirect(lst[:]))
+            nc.vector.tensor_copy(codes[:], tab[:].bitcast(U32).indirect(lst[:]))
+            return codes, scale
+
+        def first_product(name, codes, scale, fmt):
+            banks = []
+            for t in range(PACK):
+                bank = ps.tile([P, J], F32, name="%s%d" % (name, t), tag="%s%d" % (name, t))
+                nc.tensor.matmul_mx(
+                    out=bank[:],
+                    lhsT=w_codes[:, 2 * P * t : 2 * P * (t + 1)].bitcast(E2M1),
+                    lhsT_scale=w_scale[:, P * t : P * (t + 1)],
+                    rhs=codes[:].bitcast(fmt),
+                    rhs_scale=scale[:],
+                    start=True,
+                    stop=True,
+                )
+                banks.append(bank)
+            return banks
+
+        def evacuate(name, bank):
+            rows = tile(name, J, F32)
+            nc.scalar.copy(rows[:], bank[:])
+            return rows
+
+        def scatter_s(page, lst, rows):
+            nc.scalar.activation(page[:].indirect(lst[:]), rows[:], COPY)
+
+        def scatter_v(page, lst, rows):
+            nc.vector.tensor_copy(page[:].indirect(lst[:]), rows[:])
+
+        xt_codes, xt_scale = gather_packed("xt", xt_tab, xt_plane[:], l1)
+        a_ps = first_product("a", xt_codes, xt_scale, E5M2)
+        deal_scales(xo_plane, xo_stage)
+        xo_codes, xo_scale = gather_packed("xo", xo_tab, xo_plane[:], l2)
+        b_ps = first_product("b", xo_codes, xo_scale, E4M3)
+        a0 = evacuate("a_sb0", a_ps[0])
+        a1 = evacuate("a_sb1", a_ps[1])
+        scatter_s(pw[0], l3, a0)
+        scatter_v(pw[1], l3, a1)
+        a2 = evacuate("a_sb2", a_ps[2])
+        a3 = evacuate("a_sb3", a_ps[3])
+        scatter_s(pw[2], l3, a2)
+        scatter_v(pw[3], l3, a3)
+        b0 = evacuate("b_sb0", b_ps[0])
+        b1 = evacuate("b_sb1", b_ps[1])
+        scatter_s(pv[0], l4, b0)
+        scatter_v(pv[1], l4, b1)
+        b2 = evacuate("b_sb2", b_ps[2])
+        b3 = evacuate("b_sb3", b_ps[3])
+        scatter_s(pv[2], l4, b2)
+        scatter_s(pv[3], l4, b3)
+
+        hid = tile("hid", O * PACK, BF16)
+        hid_planes = hid[:].rearrange("p (o t) -> p t o", t=PACK)
+        for t in range(PACK):
+            pg = tile("pg%d" % t, C, F32)
+            nc.vector.tensor_tensor(pg[:], pw[t][:], pv[t][:], ADD)
+            nc.vector.tensor_copy(hid_planes[:, t, :], pg[:].indirect(l5[:]))
+
+        tz_rows = []
+        for h in range(2):
+            tz_tab = tile("tz_tab%d" % h, E, F32, tag=("xt_tab", "xo_tab")[h])
+            nc.sync.dma_start(tz_tab[:], tz[h * P : (h + 1) * P, :])
+            rows = tile("tz_rows%d" % h, O, F32)
+            nc.scalar.activation(rows[:], tz_tab[:].indirect(l6[:]), COPY)
+            tz_rows.append(rows)
+
+        hid_codes = tile("hid_codes", O, U32)
+        hid_scale = tile("hid_scale", O, U8)
+        nc.vector.quantize_mx(out=hid_codes[:].bitcast(E4M3), scales=hid_scale[:], in_=hid[:])
+        for h in range(2):
+            bank = ps.tile([P, O], F32, name="p%d" % h, tag="a%d" % h)
+            nc.tensor.matmul_mx(
+                out=bank[:],
+                lhsT=wb_codes[:, 2 * P * h : 2 * P * (h + 1)].bitcast(E2M1),
+                lhsT_scale=wb_plane[:, P * h : P * (h + 1)],
+                rhs=hid_codes[:].bitcast(E4M3),
+                rhs_scale=hid_scale[:],
+                start=True,
+                stop=True,
+            )
+            y = tile("y%d" % h, O, F32)
+            nc.vector.tensor_tensor(y[:], bank[:], tz_rows[h][:], ADD)
+            (nc.sync, nc.scalar)[h].dma_start(out[h * P : (h + 1) * P, :], y[:])

@@ -53,29 +53,28 @@ def tile_list_oneforboth_shared_one_tabled_kernel(
                 nc.vector.tensor_copy(words[32 * q : 32 * q + 4, :], stage[:, q * width : (q + 1) * width])
 
         xt_stage = sb.tile([4, T], I32, name="xt_stage")
-        xo_stage = sb.tile([4, Z], I32, name="xo_stage")
         w_stage = sb.tile([4, R], I32, name="w_stage")
         xt_plane = tile("xt_plane", T, U8)
         w_plane = tile("w_plane", R, U8)
         xo_plane = tile("xo_plane", Z, U8)
         wb_plane = tile("wb_plane", N, U8)
-        nc.gpsimd.memset(wb_plane[:].bitcast(I32), 0)
-        for plane in (w_plane, xt_plane, xo_plane):
+        nc.gpsimd.memset(xo_plane[:].bitcast(I32), 0)
+        for plane in (w_plane, xt_plane, wb_plane):
             nc.vector.memset(plane[:].bitcast(I32), 0)
 
         xt_tab = tile("xt_tab", T, I32)
         xo_tab = tile("xo_tab", Z, I32)
         w_raw = tile("w_raw", 2 * R, U8)
         wb_codes = tile("wb_codes", 2 * N, U8)
-        nc.scalar.dma_start(xt_tab[:], xt_words[0].rearrange("p c r -> p (c r)").bitcast(I32))
-        nc.scalar.dma_start(xo_tab[:], xo_words[0].rearrange("p c r -> p (c r)").bitcast(I32))
         load_scales_staged(w_stage, w_scales)
         load_scales_staged(xt_stage, xt_scales)
         l1 = load_list("l1", offs)
+        nc.sync.dma_start(xt_tab[:], xt_words[0].rearrange("p c r -> p (c r)").bitcast(I32))
         nc.sync.dma_start(w_raw[:].bitcast(I32), w_words[0].bitcast(I32))
-        load_scales_staged(xo_stage, xo_scales)
         l2 = load_list("l2", offs2)
+        nc.sync.dma_start(xo_tab[:], xo_words[0].rearrange("p c r -> p (c r)").bitcast(I32))
         l3 = load_list("l3", offs3)
+        load_scales_direct(xo_plane, xo_scales)
         l4 = load_list("l4", offs4)
         l5 = load_list("l5", offs5)
         l6 = load_list("l6", offs6)
@@ -83,11 +82,8 @@ def tile_list_oneforboth_shared_one_tabled_kernel(
         load_scales_direct(wb_plane, wb_scales)
 
         pw = [tile("pw%d" % t, C, F32) for t in range(PACK)]
-        pv = [tile("pv%d" % t, C, F32) for t in range(PACK)]
         for t in range(PACK):
-            nc.vector.memset(pw[t][:], 0.0)
-        for t in range(PACK):
-            nc.gpsimd.memset(pv[t][:], 0.0)
+            nc.gpsimd.memset(pw[t][:], 0.0)
 
         w_codes = tile("w_codes", 2 * R, U8)
         w_scale = tile("w_scale", R, U8)
@@ -109,21 +105,19 @@ def tile_list_oneforboth_shared_one_tabled_kernel(
             nc.vector.tensor_copy(codes[:], tab[:].bitcast(U32).indirect(lst[:]))
             return codes, scale
 
-        def first_product(name, codes, scale, fmt):
-            banks = []
-            for t in range(PACK):
-                bank = ps.tile([P, J], F32, name="%s%d" % (name, t), tag="%s%d" % (name, t))
-                nc.tensor.matmul_mx(
-                    out=bank[:],
-                    lhsT=w_codes[:, 2 * P * t : 2 * P * (t + 1)].bitcast(E2M1),
-                    lhsT_scale=w_scale[:, P * t : P * (t + 1)],
-                    rhs=codes[:].bitcast(fmt),
-                    rhs_scale=scale[:],
-                    start=True,
-                    stop=True,
-                )
-                banks.append(bank)
-            return banks
+        def first_product(dst, t, codes, scale, fmt):
+            nc.tensor.matmul_mx(
+                out=dst,
+                lhsT=w_codes[:, 2 * P * t : 2 * P * (t + 1)].bitcast(E2M1),
+                lhsT_scale=w_scale[:, P * t : P * (t + 1)],
+                rhs=codes[:].bitcast(fmt),
+                rhs_scale=scale[:],
+                start=True,
+                stop=True,
+            )
+
+        def bank_tile(name, cols):
+            return ps.tile([P, cols], F32, name=name, tag=name)
 
         def evacuate(name, bank):
             rows = tile(name, J, F32)
@@ -134,59 +128,86 @@ def tile_list_oneforboth_shared_one_tabled_kernel(
             nc.scalar.activation(page[:].indirect(lst[:]), rows[:], COPY)
 
         def scatter_v(page, lst, rows):
-            nc.vector.tensor_copy(page[:].indirect(lst[:]), rows[:])
+            nc.vector.tensor_copy(page[:].indirect(lst[:]), rows)
 
         xt_codes, xt_scale = gather_packed("xt", xt_tab, xt_plane[:], l1)
-        a_ps = first_product("a", xt_codes, xt_scale, E5M2)
-        deal_scales(xo_plane, xo_stage)
+        a_ps0, a_ps2, a_odd = bank_tile("a0", J), bank_tile("a1", J), bank_tile("a_odd", 2 * J)
+        for t, dst in ((0, a_ps0[:]), (1, a_odd[:, 0:J]), (3, a_odd[:, J : 2 * J]), (2, a_ps2[:])):
+            first_product(dst, t, xt_codes, xt_scale, E5M2)
+        pv = [tile("pv%d" % t, C, F32, tag=("w_plane", "xt_plane", "xt_scale", "xt_codes")[t]) for t in range(PACK)]
+        for t in range(PACK):
+            nc.gpsimd.memset(pv[t][:], 0.0)
         xo_codes, xo_scale = gather_packed("xo", xo_tab, xo_plane[:], l2)
-        b_ps = first_product("b", xo_codes, xo_scale, E4M3)
-        a0 = evacuate("a_sb0", a_ps[0])
-        a1 = evacuate("a_sb1", a_ps[1])
+        b_ps = [bank_tile("b%d" % t, J) for t in range(PACK)]
+        for t in range(PACK):
+            first_product(b_ps[t][:], t, xo_codes, xo_scale, E4M3)
+        a0 = evacuate("a_sb0", a_ps0)
+        a2 = evacuate("a_sb2", a_ps2)
+        a13 = tile("a_sb13", 2 * J, F32, tag="xo_plane")
+        nc.vector.tensor_copy(a13[:], a_odd[:])
         scatter_s(pw[0], l3, a0)
-        scatter_v(pw[1], l3, a1)
-        a2 = evacuate("a_sb2", a_ps[2])
-        a3 = evacuate("a_sb3", a_ps[3])
+        scatter_v(pw[1], l3, a13[:, 0:J])
         scatter_s(pw[2], l3, a2)
-        scatter_v(pw[3], l3, a3)
+        scatter_v(pw[3], l3, a13[:, J : 2 * J])
         b0 = evacuate("b_sb0", b_ps[0])
         b1 = evacuate("b_sb1", b_ps[1])
         scatter_s(pv[0], l4, b0)
-        scatter_v(pv[1], l4, b1)
+        scatter_v(pv[1], l4, b1[:])
         b2 = evacuate("b_sb2", b_ps[2])
         b3 = evacuate("b_sb3", b_ps[3])
         scatter_s(pv[2], l4, b2)
-        scatter_s(pv[3], l4, b3)
 
-        hid = tile("hid", O * PACK, BF16)
-        hid_planes = hid[:].rearrange("p (o t) -> p t o", t=PACK)
-        for t in range(PACK):
-            pg = tile("pg%d" % t, C, F32)
-            nc.vector.tensor_tensor(pg[:], pw[t][:], pv[t][:], ADD)
-            nc.vector.tensor_copy(hid_planes[:, t, :], pg[:].indirect(l5[:]))
+        planes = tile("planes", PACK * O, BF16)
+        pg = [tile("pg%d" % t, C, F32) for t in range(PACK)]
 
-        tz_rows = []
+        def add_pages(t):
+            nc.vector.tensor_tensor(pg[t][:], pw[t][:], pv[t][:], ADD)
+
+        def look_up_s(t, lo, hi):
+            nc.scalar.activation(planes[:, t * O + lo : t * O + hi], pg[t][:].indirect(l5[:, lo // 16 : hi // 16]), COPY)
+
+        def look_up_v(t, lo, hi):
+            nc.vector.tensor_copy(planes[:, t * O + lo : t * O + hi], pg[t][:].indirect(l5[:, lo // 16 : hi // 16]))
+
+        add_pages(0)
+        add_pages(1)
+        scatter_v(pv[3], l4, b3[:])
+        look_up_s(0, 0, O)
+        look_up_s(1, 0, O)
+        add_pages(2)
+        add_pages(3)
+        look_up_s(2, 0, O)
+        HALF = O // 2
+        look_up_v(3, 0, HALF)
+        look_up_s(3, HALF, O)
+
+        tz_rows = tile("tz_rows", 2 * O, F32, tag="pg3")
         for h in range(2):
             tz_tab = tile("tz_tab%d" % h, E, F32, tag=("xt_tab", "xo_tab")[h])
             nc.sync.dma_start(tz_tab[:], tz[h * P : (h + 1) * P, :])
-            rows = tile("tz_rows%d" % h, O, F32)
-            nc.scalar.activation(rows[:], tz_tab[:].indirect(l6[:]), COPY)
-            tz_rows.append(rows)
+            nc.scalar.activation(tz_rows[:, h * O : (h + 1) * O], tz_tab[:].indirect(l6[:]), COPY)
 
-        hid_codes = tile("hid_codes", O, U32)
-        hid_scale = tile("hid_scale", O, U8)
-        nc.vector.quantize_mx(out=hid_codes[:].bitcast(E4M3), scales=hid_scale[:], in_=hid[:])
-        for h in range(2):
-            bank = ps.tile([P, O], F32, name="p%d" % h, tag="a%d" % h)
-            nc.tensor.matmul_mx(
-                out=bank[:],
-                lhsT=wb_codes[:, 2 * P * h : 2 * P * (h + 1)].bitcast(E2M1),
-                lhsT_scale=wb_plane[:, P * h : P * (h + 1)],
-                rhs=hid_codes[:].bitcast(E4M3),
-                rhs_scale=hid_scale[:],
-                start=True,
-                stop=True,
-            )
-            y = tile("y%d" % h, O, F32)
-            nc.vector.tensor_tensor(y[:], bank[:], tz_rows[h][:], ADD)
-            (nc.sync, nc.scalar)[h].dma_start(out[h * P : (h + 1) * P, :], y[:])
+        hid = [tile("hid%d" % u, HALF * PACK, BF16) for u in range(2)]
+        hid_codes = [tile("hid_codes%d" % u, HALF, U32) for u in range(2)]
+        hid_scale = [tile("hid_scale%d" % u, HALF, U8) for u in range(2)]
+        by_half = planes[:].rearrange("p (t u c i) -> p u c t i", t=PACK, u=2, i=4)
+        for u in range(2):
+            nc.vector.tensor_copy(hid[u][:].rearrange("p (c i t) -> p c t i", i=4, t=PACK), by_half[:, u])
+        for u in range(2):
+            nc.vector.quantize_mx(out=hid_codes[u][:].bitcast(E4M3), scales=hid_scale[u][:], in_=hid[u][:])
+        for u in range(2):
+            bank = ps.tile([P, 2, HALF], F32, name="p%d" % u, tag="a%d" % u)
+            for h in range(2):
+                nc.tensor.matmul_mx(
+                    out=bank[:, h, :],
+                    lhsT=wb_codes[:, 2 * P * h : 2 * P * (h + 1)].bitcast(E2M1),
+                    lhsT_scale=wb_plane[:, P * h : P * (h + 1)],
+                    rhs=hid_codes[u][:].bitcast(E4M3),
+                    rhs_scale=hid_scale[u][:],
+                    start=True,
+                    stop=True,
+                )
+            y = sb.tile([P, 2, HALF], F32, name="y%d" % u)
+            cols = slice(u * HALF, (u + 1) * HALF)
+            nc.vector.tensor_tensor(y[:], bank[:], tz_rows[:].rearrange("p (h o) -> p h o", h=2)[:, :, cols], ADD)
+            (nc.sync, nc.scalar)[u].dma_start(out.rearrange("(h p) o -> p h o", h=2)[:, :, cols], y[:])

@@ -46,11 +46,10 @@ def tile_list_oneforboth_shared_one_tabled_kernel(
             rows = src[0].bitcast(I32).rearrange("(q r) c -> r q c", r=4)
             nc.sync.dma_start(stage[:].rearrange("r (q c) -> r q c", q=4), rows)
 
-        def deal_scales(plane, stage):
+        def deal_scales(plane, stage, q):
             words = plane[:].bitcast(I32)
             width = words.shape[1]
-            for q in range(4):
-                nc.vector.tensor_copy(words[32 * q : 32 * q + 4, :], stage[:, q * width : (q + 1) * width])
+            nc.vector.tensor_copy(words[32 * q : 32 * q + 4, :], stage[:, q * width : (q + 1) * width])
 
         xt_stage = sb.tile([4, T], I32, name="xt_stage")
         w_stage = sb.tile([4, R], I32, name="w_stage")
@@ -66,8 +65,8 @@ def tile_list_oneforboth_shared_one_tabled_kernel(
         xo_tab = tile("xo_tab", Z, I32)
         w_raw = tile("w_raw", 2 * R, U8)
         wb_codes = tile("wb_codes", 2 * N, U8)
-        load_scales_staged(w_stage, w_scales)
         load_scales_staged(xt_stage, xt_scales)
+        load_scales_staged(w_stage, w_scales)
         l1 = load_list("l1", offs)
         nc.sync.dma_start(xt_tab[:], xt_words[0].rearrange("p c r -> p (c r)").bitcast(I32))
         nc.sync.dma_start(w_raw[:].bitcast(I32), w_words[0].bitcast(I32))
@@ -91,8 +90,9 @@ def tile_list_oneforboth_shared_one_tabled_kernel(
             w_codes[:].bitcast(U16).rearrange("p (t m) -> p t m", t=PACK),
             w_raw[:].bitcast(U16).rearrange("p (m t) -> p t m", t=PACK),
         )
-        deal_scales(w_plane, w_stage)
-        deal_scales(xt_plane, xt_stage)
+        for q in range(4):
+            deal_scales(xt_plane, xt_stage, q)
+            deal_scales(w_plane, w_stage, q)
         nc.vector.tensor_copy(
             w_scale[:].rearrange("p (t m) -> p t m", t=PACK),
             w_plane[:].rearrange("p (m t) -> p t m", t=PACK),

@@ -119,8 +119,8 @@ def tile_list_oneforboth_shared_one_tabled_kernel(
         def bank_tile(name, cols):
             return ps.tile([P, cols], F32, name=name, tag=name)
 
-        def evacuate(name, bank):
-            rows = tile(name, J, F32)
+        def evacuate(name, bank, tag=None):
+            rows = tile(name, J, F32, tag=tag)
             nc.scalar.copy(rows[:], bank[:])
             return rows
 
@@ -131,9 +131,9 @@ def tile_list_oneforboth_shared_one_tabled_kernel(
             nc.vector.tensor_copy(page[:].indirect(lst[:]), rows)
 
         xt_codes, xt_scale = gather_packed("xt", xt_tab, xt_plane[:], l1)
-        a_ps0, a_ps2, a_odd = bank_tile("a0", J), bank_tile("a1", J), bank_tile("a_odd", 2 * J)
-        for t, dst in ((0, a_ps0[:]), (1, a_odd[:, 0:J]), (3, a_odd[:, J : 2 * J]), (2, a_ps2[:])):
-            first_product(dst, t, xt_codes, xt_scale, E5M2)
+        a_ps = [bank_tile("a%d" % t, J) for t in range(PACK)]
+        for t in range(PACK):
+            first_product(a_ps[t][:], t, xt_codes, xt_scale, E5M2)
         pv = [tile("pv%d" % t, C, F32, tag=("w_plane", "xt_plane", "xt_scale", "xt_codes")[t]) for t in range(PACK)]
         for t in range(PACK):
             nc.gpsimd.memset(pv[t][:], 0.0)
@@ -141,27 +141,29 @@ def tile_list_oneforboth_shared_one_tabled_kernel(
         b_ps = [bank_tile("b%d" % t, J) for t in range(PACK)]
         for t in range(PACK):
             first_product(b_ps[t][:], t, xo_codes, xo_scale, E4M3)
-        a0 = evacuate("a_sb0", a_ps0)
-        a2 = evacuate("a_sb2", a_ps2)
-        a13 = tile("a_sb13", 2 * J, F32, tag="xo_plane")
-        nc.vector.tensor_copy(a13[:], a_odd[:])
+        a0 = evacuate("a_sb0", a_ps[0])
+        a1 = tile("a_sb1", J, F32, tag="xo_plane")
+        nc.vector.tensor_copy(a1[:], a_ps[1][:])
         scatter_s(pw[0], l3, a0)
-        scatter_v(pw[1], l3, a13[:, 0:J])
-        scatter_s(pw[2], l3, a2)
-        scatter_v(pw[3], l3, a13[:, J : 2 * J])
-        b0 = evacuate("b_sb0", b_ps[0])
+        scatter_v(pw[1], l3, a1[:])
         b1 = evacuate("b_sb1", b_ps[1])
-        scatter_s(pv[0], l4, b0)
-        scatter_v(pv[1], l4, b1[:])
+        b0 = evacuate("b_sb0", b_ps[0])
         b2 = evacuate("b_sb2", b_ps[2])
         b3 = evacuate("b_sb3", b_ps[3])
-        scatter_s(pv[2], l4, b2)
+        scatter_s(pv[0], l4, b0)
+        scatter_v(pv[1], l4, b1[:])
+        a2 = evacuate("a_sb2", a_ps[2], tag="xo_codes")
+        a3 = evacuate("a_sb3", a_ps[3], tag="xo_scale")
+        scatter_s(pw[2], l3, a2)
+        scatter_v(pv[2], l4, b2[:])
+        scatter_s(pw[3], l3, a3)
+        scatter_v(pv[3], l4, b3[:])
 
         planes = tile("planes", PACK * O, BF16)
-        pg = [tile("pg%d" % t, C, F32) for t in range(PACK)]
+        pg = [tile("pg%d" % t, C, F32) for t in range(PACK - 1)]
 
-        def add_pages(t):
-            nc.vector.tensor_tensor(pg[t][:], pw[t][:], pv[t][:], ADD)
+        def add_pages(t, engine):
+            engine.tensor_tensor(pg[t][:], pw[t][:], pv[t][:], ADD)
 
         def look_up_s(t, lo, hi):
             nc.scalar.activation(planes[:, t * O + lo : t * O + hi], pg[t][:].indirect(l5[:, lo // 16 : hi // 16]), COPY)
@@ -169,19 +171,18 @@ def tile_list_oneforboth_shared_one_tabled_kernel(
         def look_up_v(t, lo, hi):
             nc.vector.tensor_copy(planes[:, t * O + lo : t * O + hi], pg[t][:].indirect(l5[:, lo // 16 : hi // 16]))
 
-        add_pages(0)
-        add_pages(1)
-        scatter_v(pv[3], l4, b3[:])
-        look_up_s(0, 0, O)
-        look_up_s(1, 0, O)
-        add_pages(2)
-        add_pages(3)
+        for t in (1, 0, 2):
+            add_pages(t, nc.gpsimd)
+        look_up_v(1, 0, O)
+        look_up_v(0, 0, O)
+        pg.append(tile("pg3", C, F32, tag="pg0"))
+        add_pages(3, nc.vector)
         look_up_s(2, 0, O)
         HALF = O // 2
         look_up_v(3, 0, HALF)
         look_up_s(3, HALF, O)
 
-        tz_rows = tile("tz_rows", 2 * O, F32, tag="pg3")
+        tz_rows = tile("tz_rows", 2 * O, F32, tag="pg0")
         for h in range(2):
             tz_tab = tile("tz_tab%d" % h, E, F32, tag=("xt_tab", "xo_tab")[h])
             nc.sync.dma_start(tz_tab[:], tz[h * P : (h + 1) * P, :])

@@ -14,9 +14,12 @@ E2M1 = mybir.dt.float4_e2m1fn_x4
 COPY = mybir.ActivationFunctionType.Copy
 ADD = mybir.AluOpType.add
 
-P = 128
 K, T, Z, J, R, C, O, N, E = 512, 1024, 1024, 256, 512, 512, 256, 256, 1024
+P = 128
 PACK = 4
+QUADS = 4
+PER_COLUMN = 16
+HALF = O // 2
 FLOPS = 2 * K * R * J * 2 + 2 * R * N * O
 
 
@@ -33,20 +36,20 @@ def tile_list_oneforboth_shared_one_tabled_kernel(
             return sb.tile([P, cols], dtype, name=name, tag=tag or name, align_bytes=64)
 
         def load_list(name, src):
-            lst = sb.tile([P, J // 16], U16, name=name)
+            lst = sb.tile([P, J // PER_COLUMN], U16, name=name)
             nc.sync.dma_start(lst[:], src)
             return lst
 
         def load_scales_direct(plane, src):
             rows = src[0].bitcast(I32)
-            for q in range(4):
+            for q in range(QUADS):
                 nc.sync.dma_start(plane[32 * q : 32 * q + 4, :].bitcast(I32), rows[4 * q : 4 * q + 4, :])
 
         def load_scales_staged(stage, src):
-            rows = src[0].bitcast(I32).rearrange("(q r) c -> r q c", r=4)
-            nc.sync.dma_start(stage[:].rearrange("r (q c) -> r q c", q=4), rows)
+            rows = src[0].bitcast(I32).rearrange("(q s) c -> s q c", s=4)
+            nc.sync.dma_start(stage[:].rearrange("s (q c) -> s q c", q=QUADS), rows)
 
-        def deal_scales(plane, stage, q):
+        def move_scale_rows(plane, stage, q):
             words = plane[:].bitcast(I32)
             width = words.shape[1]
             nc.vector.tensor_copy(words[32 * q : 32 * q + 4, :], stage[:, q * width : (q + 1) * width])
@@ -67,16 +70,16 @@ def tile_list_oneforboth_shared_one_tabled_kernel(
         wb_codes = tile("wb_codes", 2 * N, U8)
         load_scales_staged(xt_stage, xt_scales)
         load_scales_staged(w_stage, w_scales)
-        l1 = load_list("l1", offs)
-        nc.sync.dma_start(xt_tab[:], xt_words[0].rearrange("p c r -> p (c r)").bitcast(I32))
+        token_list = load_list("token_list", offs)
+        note_list = load_list("note_list", offs2)
         nc.sync.dma_start(w_raw[:].bitcast(I32), w_words[0].bitcast(I32))
-        l2 = load_list("l2", offs2)
+        nc.sync.dma_start(xt_tab[:], xt_words[0].rearrange("p c r -> p (c r)").bitcast(I32))
         nc.sync.dma_start(xo_tab[:], xo_words[0].rearrange("p c r -> p (c r)").bitcast(I32))
-        l3 = load_list("l3", offs3)
+        a_places = load_list("a_places", offs3)
         load_scales_direct(xo_plane, xo_scales)
-        l4 = load_list("l4", offs4)
-        l5 = load_list("l5", offs5)
-        l6 = load_list("l6", offs6)
+        b_places = load_list("b_places", offs4)
+        read_list = load_list("read_list", offs5)
+        entry_list = load_list("entry_list", offs6)
         nc.sync.dma_start(wb_codes[:].bitcast(I32), wb_words[0].bitcast(I32))
         load_scales_direct(wb_plane, wb_scales)
 
@@ -90,108 +93,108 @@ def tile_list_oneforboth_shared_one_tabled_kernel(
             w_codes[:].bitcast(U16).rearrange("p (t m) -> p t m", t=PACK),
             w_raw[:].bitcast(U16).rearrange("p (m t) -> p t m", t=PACK),
         )
-        for q in range(4):
-            deal_scales(xt_plane, xt_stage, q)
-            deal_scales(w_plane, w_stage, q)
-        nc.vector.tensor_copy(
-            w_scale[:].rearrange("p (t m) -> p t m", t=PACK),
-            w_plane[:].rearrange("p (m t) -> p t m", t=PACK),
-        )
+        for q in range(QUADS):
+            move_scale_rows(xt_plane, xt_stage, q)
+            move_scale_rows(w_plane, w_stage, q)
+        for lo, hi in ((0, 1), (1, 2), (2, PACK)):
+            nc.gpsimd.tensor_copy(
+                w_scale[:].rearrange("p (t m) -> p t m", t=PACK)[:, lo:hi, :],
+                w_plane[:].rearrange("p (m t) -> p t m", t=PACK)[:, lo:hi, :],
+            )
 
         def gather_packed(name, tab, plane, lst):
             codes = tile(name + "_codes", J, U32)
             scale = tile(name + "_scale", J, U8)
-            nc.vector.tensor_copy(scale[:], plane.indirect(lst[:]))
+            nc.vector.tensor_copy(scale[:], plane[:].indirect(lst[:]))
             nc.vector.tensor_copy(codes[:], tab[:].bitcast(U32).indirect(lst[:]))
             return codes, scale
 
-        def first_product(dst, t, codes, scale, fmt):
-            nc.tensor.matmul_mx(
-                out=dst,
-                lhsT=w_codes[:, 2 * P * t : 2 * P * (t + 1)].bitcast(E2M1),
-                lhsT_scale=w_scale[:, P * t : P * (t + 1)],
-                rhs=codes[:].bitcast(fmt),
-                rhs_scale=scale[:],
-                start=True,
-                stop=True,
-            )
+        def first_product(name, codes, scale, fmt):
+            banks = [ps.tile([P, J], F32, name="%s%d" % (name, t), tag="%s%d" % (name, t)) for t in range(PACK)]
+            for t in range(PACK):
+                nc.tensor.matmul_mx(
+                    out=banks[t][:],
+                    lhsT=w_codes[:, 2 * P * t : 2 * P * (t + 1)].bitcast(E2M1),
+                    lhsT_scale=w_scale[:, P * t : P * (t + 1)],
+                    rhs=codes[:].bitcast(fmt),
+                    rhs_scale=scale[:],
+                    start=True,
+                    stop=True,
+                )
+            return banks
 
-        def bank_tile(name, cols):
-            return ps.tile([P, cols], F32, name=name, tag=name)
-
-        def evacuate(name, bank, tag=None):
+        def copy_out_on_scalar(name, bank, tag=None):
             rows = tile(name, J, F32, tag=tag)
             nc.scalar.copy(rows[:], bank[:])
             return rows
 
-        def scatter_s(page, lst, rows):
+        def scatter_on_scalar(page, lst, rows):
             nc.scalar.activation(page[:].indirect(lst[:]), rows[:], COPY)
 
-        def scatter_v(page, lst, rows):
-            nc.vector.tensor_copy(page[:].indirect(lst[:]), rows)
+        def scatter_on_vector(page, lst, rows):
+            nc.vector.tensor_copy(page[:].indirect(lst[:]), rows[:])
 
-        xt_codes, xt_scale = gather_packed("xt", xt_tab, xt_plane[:], l1)
-        a_ps = [bank_tile("a%d" % t, J) for t in range(PACK)]
-        for t in range(PACK):
-            first_product(a_ps[t][:], t, xt_codes, xt_scale, E5M2)
+        xt_codes, xt_scale = gather_packed("xt", xt_tab, xt_plane, token_list)
+        a_ps = first_product("a", xt_codes, xt_scale, E5M2)
         pv = [tile("pv%d" % t, C, F32, tag=("w_plane", "xt_plane", "xt_scale", "xt_codes")[t]) for t in range(PACK)]
-        for t in range(PACK):
+        for t in (1, 0, 2, 3):
             nc.gpsimd.memset(pv[t][:], 0.0)
-        xo_codes, xo_scale = gather_packed("xo", xo_tab, xo_plane[:], l2)
-        b_ps = [bank_tile("b%d" % t, J) for t in range(PACK)]
-        for t in range(PACK):
-            first_product(b_ps[t][:], t, xo_codes, xo_scale, E4M3)
-        a0 = evacuate("a_sb0", a_ps[0])
+        xo_codes, xo_scale = gather_packed("xo", xo_tab, xo_plane, note_list)
+        b_ps = first_product("b", xo_codes, xo_scale, E4M3)
+
+        a0 = copy_out_on_scalar("a_sb0", a_ps[0])
         a1 = tile("a_sb1", J, F32, tag="xo_plane")
         nc.vector.tensor_copy(a1[:], a_ps[1][:])
-        scatter_s(pw[0], l3, a0)
-        scatter_v(pw[1], l3, a1[:])
-        b1 = evacuate("b_sb1", b_ps[1])
-        b0 = evacuate("b_sb0", b_ps[0])
-        b2 = evacuate("b_sb2", b_ps[2])
-        b3 = evacuate("b_sb3", b_ps[3])
-        scatter_s(pv[0], l4, b0)
-        scatter_v(pv[1], l4, b1[:])
-        a2 = evacuate("a_sb2", a_ps[2], tag="xo_codes")
-        a3 = evacuate("a_sb3", a_ps[3], tag="xo_scale")
-        scatter_s(pw[2], l3, a2)
-        scatter_v(pv[2], l4, b2[:])
-        scatter_s(pw[3], l3, a3)
-        scatter_v(pv[3], l4, b3[:])
+        scatter_on_scalar(pw[0], a_places, a0)
+        scatter_on_vector(pw[1], a_places, a1)
+        b1 = copy_out_on_scalar("b_sb1", b_ps[1])
+        b0 = copy_out_on_scalar("b_sb0", b_ps[0])
+        b2 = copy_out_on_scalar("b_sb2", b_ps[2])
+        b3 = copy_out_on_scalar("b_sb3", b_ps[3])
+        scatter_on_scalar(pv[0], b_places, b0)
+        scatter_on_vector(pv[1], b_places, b1)
+        a2 = copy_out_on_scalar("a_sb2", a_ps[2], tag="xo_codes")
+        a3 = copy_out_on_scalar("a_sb3", a_ps[3], tag="xo_scale")
+        scatter_on_scalar(pw[2], a_places, a2)
+        scatter_on_vector(pv[2], b_places, b2)
+        scatter_on_scalar(pw[3], a_places, a3)
+        scatter_on_vector(pv[3], b_places, b3)
 
-        planes = tile("planes", PACK * O, BF16)
+        hid_slices = tile("hid_slices", PACK * O, BF16)
         pg = [tile("pg%d" % t, C, F32) for t in range(PACK - 1)]
 
         def add_pages(t, engine):
             engine.tensor_tensor(pg[t][:], pw[t][:], pv[t][:], ADD)
 
-        def look_up_s(t, lo, hi):
-            nc.scalar.activation(planes[:, t * O + lo : t * O + hi], pg[t][:].indirect(l5[:, lo // 16 : hi // 16]), COPY)
+        def listed_board(t, lo, hi):
+            return pg[t][:].indirect(read_list[:, lo // PER_COLUMN : hi // PER_COLUMN])
 
-        def look_up_v(t, lo, hi):
-            nc.vector.tensor_copy(planes[:, t * O + lo : t * O + hi], pg[t][:].indirect(l5[:, lo // 16 : hi // 16]))
+        def look_up_on_scalar(t, lo, hi):
+            nc.scalar.activation(hid_slices[:, t * O + lo : t * O + hi], listed_board(t, lo, hi), COPY)
+
+        def look_up_on_vector(t, lo, hi):
+            nc.vector.tensor_copy(hid_slices[:, t * O + lo : t * O + hi], listed_board(t, lo, hi))
 
         for t in (1, 0, 2):
             add_pages(t, nc.gpsimd)
-        look_up_v(1, 0, O)
-        look_up_v(0, 0, O)
-        pg.append(tile("pg3", C, F32, tag="pg0"))
+        look_up_on_vector(1, 0, O)
+        look_up_on_vector(0, 0, O)
+        pg.append(tile("pg3", C, F32, tag="pw2"))
         add_pages(3, nc.vector)
-        look_up_s(2, 0, O)
-        HALF = O // 2
-        look_up_v(3, 0, HALF)
-        look_up_s(3, HALF, O)
+        look_up_on_scalar(2, 0, O)
+        look_up_on_vector(3, 0, HALF)
+        look_up_on_scalar(3, HALF, O)
 
-        tz_rows = tile("tz_rows", 2 * O, F32, tag="pg0")
+        tz_rows = tile("tz_rows", 2 * O, F32, tag="pw2")
         for h in range(2):
             tz_tab = tile("tz_tab%d" % h, E, F32, tag=("xt_tab", "xo_tab")[h])
             nc.sync.dma_start(tz_tab[:], tz[h * P : (h + 1) * P, :])
-            nc.scalar.activation(tz_rows[:, h * O : (h + 1) * O], tz_tab[:].indirect(l6[:]), COPY)
+            nc.scalar.activation(tz_rows[:, h * O : (h + 1) * O], tz_tab[:].indirect(entry_list[:]), COPY)
 
         hid = [tile("hid%d" % u, HALF * PACK, BF16) for u in range(2)]
         hid_codes = [tile("hid_codes%d" % u, HALF, U32) for u in range(2)]
         hid_scale = [tile("hid_scale%d" % u, HALF, U8) for u in range(2)]
-        by_half = planes[:].rearrange("p (t u c i) -> p u c t i", t=PACK, u=2, i=4)
+        by_half = hid_slices[:].rearrange("p (t u c i) -> p u c t i", t=PACK, u=2, i=4)
         for u in range(2):
             nc.vector.tensor_copy(hid[u][:].rearrange("p (c i t) -> p c t i", i=4, t=PACK), by_half[:, u])
         for u in range(2):

from contextlib import ExitStack

import concourse.mybir as mybir

F32 = mybir.dt.float32
BF16 = mybir.dt.bfloat16
I32 = mybir.dt.int32
U32 = mybir.dt.uint32
U16 = mybir.dt.uint16
U8 = mybir.dt.uint8
E4M3 = mybir.dt.float8_e4m3fn_x4
E5M2 = mybir.dt.float8_e5m2_x4
E2M1 = mybir.dt.float4_e2m1fn_x4
COPY = mybir.ActivationFunctionType.Copy
ADD = mybir.AluOpType.add

K, T, Z, J, R, C, O, N, E = 512, 1024, 1024, 256, 512, 512, 256, 256, 1024
P = 128
PACK = 4
QUADS = 4
PER_COLUMN = 16
HALF = O // 2
FLOPS = 2 * K * R * J * 2 + 2 * R * N * O


def tile_list_oneforboth_shared_one_tabled_kernel(
    tc, xt_words, xt_scales, xo_words, xo_scales, w_words, w_scales, wb_words, wb_scales, tz,
    offs, offs2, offs3, offs4, offs5, offs6, out,
):
    nc = tc.nc
    with ExitStack() as ctx:
        sb = ctx.enter_context(tc.tile_pool(name="sb", bufs=1))
        ps = ctx.enter_context(tc.psum_pool(name="ps", bufs=1))

        def tile(name, cols, dtype, tag=None):
            return sb.tile([P, cols], dtype, name=name, tag=tag or name, align_bytes=64)

        def load_list(name, src):
            lst = sb.tile([P, J // PER_COLUMN], U16, name=name)
            nc.sync.dma_start(lst[:], src)
            return lst

        def load_scales_direct(plane, src):
            rows = src[0].bitcast(I32)
            for q in range(QUADS):
                nc.sync.dma_start(plane[32 * q : 32 * q + 4, :].bitcast(I32), rows[4 * q : 4 * q + 4, :])

        def load_scales_staged(stage, src):
            rows = src[0].bitcast(I32).rearrange("(q s) c -> s q c", s=4)
            nc.sync.dma_start(stage[:].rearrange("s (q c) -> s q c", q=QUADS), rows)

        def move_scale_rows(plane, stage, q):
            words = plane[:].bitcast(I32)
            width = words.shape[1]
            nc.vector.tensor_copy(words[32 * q : 32 * q + 4, :], stage[:, q * width : (q + 1) * width])

        xt_stage = sb.tile([4, T], I32, name="xt_stage")
        w_stage = sb.tile([4, R], I32, name="w_stage")
        xt_plane = tile("xt_plane", T, U8)
        w_plane = tile("w_plane", R, U8)
        xo_plane = tile("xo_plane", Z, U8)
        wb_plane = tile("wb_plane", N, U8)
        nc.gpsimd.memset(xo_plane[:].bitcast(I32), 0)
        for plane in (w_plane, xt_plane, wb_plane):
            nc.vector.memset(plane[:].bitcast(I32), 0)

        xt_tab = tile("xt_tab", T, I32)
        xo_tab = tile("xo_tab", Z, I32)
        w_raw = tile("w_raw", 2 * R, U8)
        wb_codes = tile("wb_codes", 2 * N, U8)
        load_scales_staged(xt_stage, xt_scales)
        load_scales_staged(w_stage, w_scales)
        token_list = load_list("token_list", offs)
        note_list = load_list("note_list", offs2)
        nc.sync.dma_start(w_raw[:].bitcast(I32), w_words[0].bitcast(I32))
        nc.sync.dma_start(xt_tab[:], xt_words[0].rearrange("p c r -> p (c r)").bitcast(I32))
        nc.sync.dma_start(xo_tab[:], xo_words[0].rearrange("p c r -> p (c r)").bitcast(I32))
        a_places = load_list("a_places", offs3)
        load_scales_direct(xo_plane, xo_scales)
        b_places = load_list("b_places", offs4)
        read_list = load_list("read_list", offs5)
        entry_list = load_list("entry_list", offs6)
        nc.sync.dma_start(wb_codes[:].bitcast(I32), wb_words[0].bitcast(I32))
        load_scales_direct(wb_plane, wb_scales)

        pw = [tile("pw%d" % t, C, F32) for t in range(PACK)]
        for t in range(PACK):
            nc.gpsimd.memset(pw[t][:], 0.0)

        w_codes = tile("w_codes", 2 * R, U8)
        w_scale = tile("w_scale", R, U8)
        nc.scalar.copy(
            w_codes[:].bitcast(U16).rearrange("p (t m) -> p t m", t=PACK),
            w_raw[:].bitcast(U16).rearrange("p (m t) -> p t m", t=PACK),
        )
        for q in range(QUADS):
            move_scale_rows(xt_plane, xt_stage, q)
            move_scale_rows(w_plane, w_stage, q)
        for lo, hi in ((0, 1), (1, 2), (2, PACK)):
            nc.gpsimd.tensor_copy(
                w_scale[:].rearrange("p (t m) -> p t m", t=PACK)[:, lo:hi, :],
                w_plane[:].rearrange("p (m t) -> p t m", t=PACK)[:, lo:hi, :],
            )

        def gather_packed(name, tab, plane, lst):
            codes = tile(name + "_codes", J, U32)
            scale = tile(name + "_scale", J, U8)
            nc.vector.tensor_copy(scale[:], plane[:].indirect(lst[:]))
            nc.vector.tensor_copy(codes[:], tab[:].bitcast(U32).indirect(lst[:]))
            return codes, scale

        def first_product(name, codes, scale, fmt):
            banks = [ps.tile([P, J], F32, name="%s%d" % (name, t), tag="%s%d" % (name, t)) for t in range(PACK)]
            for t in range(PACK):
                nc.tensor.matmul_mx(
                    out=banks[t][:],
                    lhsT=w_codes[:, 2 * P * t : 2 * P * (t + 1)].bitcast(E2M1),
                    lhsT_scale=w_scale[:, P * t : P * (t + 1)],
                    rhs=codes[:].bitcast(fmt),
                    rhs_scale=scale[:],
                    start=True,
                    stop=True,
                )
            return banks

        def copy_out_on_scalar(name, bank, tag=None):
            rows = tile(name, J, F32, tag=tag)
            nc.scalar.copy(rows[:], bank[:])
            return rows

        def scatter_on_scalar(page, lst, rows):
            nc.scalar.activation(page[:].indirect(lst[:]), rows[:], COPY)

        def scatter_on_vector(page, lst, rows):
            nc.vector.tensor_copy(page[:].indirect(lst[:]), rows[:])

        xt_codes, xt_scale = gather_packed("xt", xt_tab, xt_plane, token_list)
        a_ps = first_product("a", xt_codes, xt_scale, E5M2)
        pv = [tile("pv%d" % t, C, F32, tag=("w_plane", "xt_plane", "xt_scale", "xt_codes")[t]) for t in range(PACK)]
        for t in (1, 0, 2, 3):
            nc.gpsimd.memset(pv[t][:], 0.0)
        xo_codes, xo_scale = gather_packed("xo", xo_tab, xo_plane, note_list)
        b_ps = first_product("b", xo_codes, xo_scale, E4M3)

        a0 = copy_out_on_scalar("a_sb0", a_ps[0])
        a1 = tile("a_sb1", J, F32, tag="xo_plane")
        nc.vector.tensor_copy(a1[:], a_ps[1][:])
        scatter_on_scalar(pw[0], a_places, a0)
        scatter_on_vector(pw[1], a_places, a1)
        b1 = copy_out_on_scalar("b_sb1", b_ps[1])
        b0 = copy_out_on_scalar("b_sb0", b_ps[0])
        b2 = copy_out_on_scalar("b_sb2", b_ps[2])
        b3 = copy_out_on_scalar("b_sb3", b_ps[3])
        scatter_on_scalar(pv[0], b_places, b0)
        scatter_on_vector(pv[1], b_places, b1)
        a2 = copy_out_on_scalar("a_sb2", a_ps[2], tag="xo_codes")
        a3 = copy_out_on_scalar("a_sb3", a_ps[3], tag="xo_scale")
        scatter_on_scalar(pw[2], a_places, a2)
        scatter_on_vector(pv[2], b_places, b2)
        scatter_on_scalar(pw[3], a_places, a3)
        scatter_on_vector(pv[3], b_places, b3)

        hid_slices = tile("hid_slices", PACK * O, BF16)
        pg = [tile("pg%d" % t, C, F32) for t in range(PACK - 1)]

        def add_pages(t, engine):
            engine.tensor_tensor(pg[t][:], pw[t][:], pv[t][:], ADD)

        def listed_board(t, lo, hi):
            return pg[t][:].indirect(read_list[:, lo // PER_COLUMN : hi // PER_COLUMN])

        def look_up_on_scalar(t, lo, hi):
            nc.scalar.activation(hid_slices[:, t * O + lo : t * O + hi], listed_board(t, lo, hi), COPY)

        def look_up_on_vector(t, lo, hi):
            nc.vector.tensor_copy(hid_slices[:, t * O + lo : t * O + hi], listed_board(t, lo, hi))

        for t in (1, 0, 2):
            add_pages(t, nc.gpsimd)
        look_up_on_vector(1, 0, O)
        look_up_on_vector(0, 0, O)
        pg.append(tile("pg3", C, F32, tag="pw2"))
        add_pages(3, nc.vector)
        look_up_on_scalar(2, 0, O)
        look_up_on_vector(3, 0, HALF)
        look_up_on_scalar(3, HALF, O)

        tz_rows = tile("tz_rows", 2 * O, F32, tag="pw2")
        for h in range(2):
            tz_tab = tile("tz_tab%d" % h, E, F32, tag=("xt_tab", "xo_tab")[h])
            nc.sync.dma_start(tz_tab[:], tz[h * P : (h + 1) * P, :])
            nc.scalar.activation(tz_rows[:, h * O : (h + 1) * O], tz_tab[:].indirect(entry_list[:]), COPY)

        hid = [tile("hid%d" % u, HALF * PACK, BF16) for u in range(2)]
        hid_codes = [tile("hid_codes%d" % u, HALF, U32) for u in range(2)]
        hid_scale = [tile("hid_scale%d" % u, HALF, U8) for u in range(2)]
        by_half = hid_slices[:].rearrange("p (t u c i) -> p u c t i", t=PACK, u=2, i=4)
        for u in range(2):
            nc.vector.tensor_copy(hid[u][:].rearrange("p (c i t) -> p c t i", i=4, t=PACK), by_half[:, u])
        for u in range(2):
            nc.vector.quantize_mx(out=hid_codes[u][:].bitcast(E4M3), scales=hid_scale[u][:], in_=hid[u][:])
        for u in range(2):
            bank = ps.tile([P, 2, HALF], F32, name="p%d" % u, tag="a%d" % u)
            for h in range(2):
                nc.tensor.matmul_mx(
                    out=bank[:, h, :],
                    lhsT=wb_codes[:, 2 * P * h : 2 * P * (h + 1)].bitcast(E2M1),
                    lhsT_scale=wb_plane[:, P * h : P * (h + 1)],
                    rhs=hid_codes[u][:].bitcast(E4M3),
                    rhs_scale=hid_scale[u][:],
                    start=True,
                    stop=True,
                )
            y = sb.tile([P, 2, HALF], F32, name="y%d" % u)
            cols = slice(u * HALF, (u + 1) * HALF)
            nc.vector.tensor_tensor(y[:], bank[:], tz_rows[:].rearrange("p (h o) -> p h o", h=2)[:, :, cols], ADD)
            (nc.sync, nc.scalar)[u].dma_start(out.rearrange("(h p) o -> p h o", h=2)[:, :, cols], y[:])
